import numpy as np
import ml_dtypes


def mxq(x, axis, fmt="e4m3"):
    dtype, down = {"e4m3": (ml_dtypes.float8_e4m3fn, 7), "e5m2": (ml_dtypes.float8_e5m2, 14)}[fmt]
    v = np.moveaxis(np.asarray(x, np.float32).astype(ml_dtypes.bfloat16).astype(np.float64), axis, -1)
    blocks = v.reshape(v.shape[:-1] + (-1, 32))
    amax = np.abs(blocks).max(-1, keepdims=True)
    byte = np.maximum(np.where(amax > 0, np.frexp(amax)[1] - 1 + 127, 0) - down, 1)
    scale = np.exp2(byte - 127.0)
    codes = (blocks / scale).astype(np.float32).astype(dtype).astype(np.float64)
    return np.moveaxis((codes * scale).reshape(v.shape), -1, axis)


WIDE = False


def mx_kscale(k):
    if not WIDE:
        return np.ones(k)
    levels = np.array([10, -10, 5, -5, 0])
    if k % 512:
        return np.exp2(np.random.permutation(np.resize(levels, k // 32))).repeat(32)
    a = np.empty((k // 512, 16))
    for p in range(k // 512):
        a[p, :8] = np.random.permutation(np.resize(levels, 8))
        for g in range(8):
            far = levels[np.abs(levels - a[p, g]) >= 10]
            a[p, g + 8] = far[np.random.randint(len(far))]
    return np.exp2(a.ravel()).repeat(32)


def f64(x):
    return np.asarray(x).astype(np.float64)


def striped(idx):
    return np.tile(idx.reshape(-1, 16).T, (8, 1)).astype(np.uint16)


def unstriped(offs):
    return offs[:16].T.reshape(-1).astype(np.int64)


def pack_weight(w):
    k, n = w.shape
    w = f64(np.asarray(w, np.float32).astype(ml_dtypes.bfloat16)).reshape(k // 32, 32, n)
    amax = np.abs(w).max(1)
    byte = np.clip(np.where(amax > 0, np.frexp(amax)[1] - 1 + 127 - 7, 1), 1, 254)
    scaled = (w * np.exp2(127.0 - byte)[:, None, :]).reshape(k, n).astype(np.float32)
    words = np.ascontiguousarray(scaled.reshape(k // 512, 128, 4, n).transpose(0, 1, 3, 2)).astype(ml_dtypes.float8_e4m3fn).view(np.uint8)
    return words, np.ascontiguousarray(byte.astype(np.uint8).reshape(k // 512, 16, n))


def unpack_weight(words, scales):
    g, p, n, _ = words.shape
    vals = np.ascontiguousarray(words).view(ml_dtypes.float8_e4m3fn).astype(np.float64) * np.repeat(np.exp2(scales.astype(np.float64) - 127.0), 8, axis=1)[..., None]
    return vals.transpose(0, 1, 3, 2).reshape(g * 512, n)


K, T, S, D, N = 512, 2048, 1024, 4, 128
P = 2 ** 7


def setup_inputs():
    n = np.random.standard_normal
    s = mx_kscale(K)[:, None]
    packed_xT = pack_weight(n((K, T)) * s)
    return {
        "x_words": packed_xT[0],
        "x_scales": packed_xT[1],
        "w1": (n((K, N)) / np.sqrt(K) / s).astype(np.float32),
        "w2": (n((K, N)) / np.sqrt(K) / s).astype(np.float32),
        "ago": (np.tile(np.random.uniform(0.1, 2.5, S), (P, 1))).astype(np.float32),
        "amt": (np.tile(np.random.uniform(0.5, 2.0, S), (P, 1))).astype(np.float32),
        "offs": striped(np.random.permutation(T)[:S]),
    }


def reference(x_words, x_scales, w1, w2, ago, amt, offs):
    xq = unpack_weight(x_words, x_scales)[:, unstriped(offs)]
    ya = mxq(f64(w1), 0, "e4m3").T @ xq
    fast = np.log(np.exp(ya) + 1.0) + 0.4
    ef = np.exp(-1.0 * (fast * f64(ago)[:1]))
    yb = mxq(f64(w2), 0, "e4m3").T @ xq
    slow = 0.4 * (np.log(np.exp(yb) + 1.0))
    es = np.exp(-1.0 * (slow * f64(ago)[:1]))
    cd = f64(amt)[:1] * (0.7 * ef + 0.3 * es)
    conc = cd.reshape(len(cd), -1, D).sum(axis=2)
    auc = f64(amt)[:1] * ((-1.0 * ef + 1.0) / fast)
    return np.log(conc + 0.05) - (0.5 * (auc.reshape(len(auc), -1, D).max(axis=2)))

@@ -1,0 +1,142 @@
+import math
+from contextlib import ExitStack
+
+import concourse.mybir as mybir
+from concourse.masks import make_identity
+
+K, T, S, D, N = 512, 2048, 1024, 4, 128
+FLOPS = 2 * 2 * K * N * S
+BYTES = K * T + K // 32 * T + 2 * K * N * 4 + 2 * S * 4 + 128 * S // 16 * 2 + N * S // D * 4
+
+F32 = mybir.dt.float32
+BF16 = mybir.dt.bfloat16
+I32 = mybir.dt.int32
+U32 = mybir.dt.uint32
+U16 = mybir.dt.uint16
+U8 = mybir.dt.uint8
+FP8X4 = mybir.dt.float8_e4m3fn_x4
+ACT = mybir.ActivationFunctionType
+ALU = mybir.AluOpType
+AX = mybir.AxisListType
+
+P = 128
+PACK = 4
+TILES = S // P
+CHUNK = 256
+CHUNKS = S // CHUNK
+HALF = 512
+LN_FLOOR = 2.0 ** -62
+RECIP_V = 32
+
+
+def tile_picked_ypkpd_logc_p_kernel(tc, x_words, x_scales, w1, w2, ago, amt, offs, out):
+    nc = tc.nc
+    with ExitStack() as ctx:
+        keep = ctx.enter_context(tc.tile_pool(name="keep", bufs=1))
+        psum = ctx.enter_context(tc.psum_pool(name="psum", bufs=1))
+
+        offsets = keep.tile([P, S // 16], U16, name="offsets")
+        scale_table = keep.tile([P, T], U8, name="scale_table", align_bytes=64)
+        word_table = keep.tile([P, T], U32, name="word_table", align_bytes=64)
+        w_raw = [keep.tile([P, PACK, N], F32, name="w_raw%d" % h) for h in range(2)]
+        ago_col = keep.tile([P, TILES], F32, name="ago_col")
+        amt_col = keep.tile([P, TILES], F32, name="amt_col")
+
+        nc.vector.memset(scale_table[:].bitcast(I32), 0)
+        for q in range(4):
+            nc.sync.dma_start(scale_table[32 * q : 32 * q + 4, :].bitcast(I32), x_scales[0, 4 * q : 4 * q + 4, :].bitcast(I32))
+        nc.sync.dma_start(offsets[:], offs)
+        for h, w in enumerate((w1, w2)):
+            nc.sync.dma_start(w_raw[h][:], w.rearrange("(p j) n -> p j n", j=PACK))
+        nc.sync.dma_start(word_table[:].bitcast(I32), x_words[0].rearrange("p c r -> p (c r)").bitcast(I32))
+        with nc.allow_non_contiguous_dma(reason="one value a partition and tile"):
+            nc.sync.dma_start(ago_col[:], ago[0].rearrange("(t p) -> p t", p=P))
+            nc.sync.dma_start(amt_col[:], amt[0].rearrange("(t p) -> p t", p=P))
+
+        warm_in = keep.tile([P, 1], F32, name="warm_in")
+        warm_out = keep.tile([P, 1], F32, name="warm_out")
+        nc.gpsimd.memset(warm_in[:], 0.0)
+        nc.scalar.activation(warm_out[:], warm_in[:], ACT.Sigmoid)
+
+        ident = keep.tile([P, P], F32, name="ident")
+        make_identity(nc, ident[:])
+
+        w_bf = keep.tile([P, 2, N, PACK], BF16, name="w_bf", align_bytes=64)
+        for h in range(2):
+            nc.scalar.activation(w_bf[:, h, :, :], w_raw[h][:].rearrange("p j n -> p n j"), ACT.Copy)
+        w_codes = keep.tile([P, 2 * N], U32, name="w_codes", align_bytes=64)
+        w_scales = keep.tile([P, 2 * N], U8, name="w_scales", align_bytes=64)
+
+        x_scale = keep.tile([P, S], U8, name="x_scale", align_bytes=64)
+        nc.vector.tensor_copy(x_scale[:], scale_table[:].indirect(offsets[:]))
+        nc.vector.quantize_mx(out=w_codes[:].bitcast(FP8X4), scales=w_scales[:], in_=w_bf[:].rearrange("p h n j -> p (h n j)"))
+
+        neg_ago = keep.tile([P, TILES], F32, name="neg_ago")
+        neg_ago4 = keep.tile([P, TILES], F32, name="neg_ago4")
+        nc.gpsimd.tensor_scalar(neg_ago[:], ago_col[:], -1.0, 0.0, ALU.mult, ALU.add)
+        nc.gpsimd.tensor_scalar(neg_ago4[:], ago_col[:], -0.4, 0.0, ALU.mult, ALU.add)
+
+        u = keep.tile([P, 2, TILES, N], F32, name="u")
+        y = []
+        for c in range(CHUNKS):
+            x_code = keep.tile([P, CHUNK], U32, name="x_code%d" % c, align_bytes=64)
+            nc.vector.tensor_copy(x_code[:], word_table[:].indirect(offsets[:, c * CHUNK // 16 : (c + 1) * CHUNK // 16]))
+            bank = psum.tile([P, 2, 2, N], F32, name="y%d" % c)
+            y.append(bank)
+            for i in range(2):
+                nc.tensor.matmul_mx(
+                    out=bank[:, i, :, :].rearrange("p h n -> p (h n)"),
+                    lhsT=x_code[:, i * P : (i + 1) * P].bitcast(FP8X4),
+                    lhsT_scale=x_scale[:, c * CHUNK + i * P : c * CHUNK + (i + 1) * P],
+                    rhs=w_codes[:].bitcast(FP8X4),
+                    rhs_scale=w_scales[:],
+                    start=True,
+                    stop=True,
+                )
+            nc.scalar.activation(u[:, :, 2 * c : 2 * c + 2, :].rearrange("p h i n -> p i h n"), bank[:], ACT.Sigmoid, scale=-1.0)
+
+        for h in range(2):
+            nc.scalar.activation(u[:, h, :, :], u[:, h, :, :], ACT.Ln, bias=LN_FLOOR)
+        for h in range(2):
+            for c in range(CHUNKS):
+                piece = u[:, h, 2 * c : 2 * c + 2, :]
+                nc.vector.scalar_tensor_tensor(piece, piece, -1.0, y[c][:, :, h, :], ALU.mult, ALU.max)
+
+        inv = keep.tile([P, TILES, N], F32, name="inv")
+        fast_v = keep.tile([P, TILES, RECIP_V], F32, name="fast_v")
+        ln_fast = keep.tile([P, TILES, N - RECIP_V], F32, name="ln_fast")
+        nc.scalar.activation(ln_fast[:], u[:, 0, :, RECIP_V:], ACT.Ln, bias=0.4)
+        nc.vector.tensor_scalar(fast_v[:], u[:, 0, :, :RECIP_V], 0.4, None, ALU.add)
+        nc.vector.reciprocal(inv[:, :, :RECIP_V], fast_v[:])
+
+        scaled = keep.tile([P, TILES, 2, N], F32, name="scaled")
+        neg_auc = keep.tile([P, TILES, N], F32, name="neg_auc")
+        conc = keep.tile([P, S // D], F32, name="conc")
+        least = keep.tile([P, S // D], F32, name="least")
+        per_half = TILES // 2
+        for half in range(2):
+            dose_t = psum.tile([P, HALF], F32, name="dose_t%d" % half)
+            auc_t = psum.tile([P, HALF], F32, name="auc_t%d" % half)
+            for i in range(per_half):
+                t = half * per_half + i
+                col = slice(t, t + 1)
+                nc.scalar.activation(u[:, 0, t, :], u[:, 0, t, :], ACT.Exp, scale=neg_ago[:, col], bias=neg_ago4[:, col])
+                nc.scalar.activation(u[:, 1, t, :], u[:, 1, t, :], ACT.Exp, scale=neg_ago4[:, col], bias=math.log(0.3 / 0.7))
+                if i == 0:
+                    tiles = slice(half * per_half, (half + 1) * per_half)
+                    nc.scalar.activation(inv[:, tiles, RECIP_V:], ln_fast[:, tiles, :], ACT.Exp, scale=-1.0)
+                nc.vector.tensor_scalar(scaled[:, t, :, :], u[:, :, t, :], amt_col[:, col], None, ALU.mult)
+                nc.vector.scalar_tensor_tensor(neg_auc[:, t, :], scaled[:, t, 0, :], amt_col[:, col], inv[:, t, :], ALU.subtract, ALU.mult)
+                cols = slice(i * P, (i + 1) * P)
+                for h in range(2):
+                    nc.tensor.matmul(dose_t[:, cols], scaled[:, t, h, :], ident[:], start=(h == 0), stop=(h == 1), is_transpose=True)
+                nc.tensor.transpose(auc_t[:, cols], neg_auc[:, t, :], ident[:])
+            v = slice(half * P, (half + 1) * P)
+            nc.vector.tensor_reduce(conc[:, v], dose_t[:].rearrange("p (v d) -> p v d", d=D), AX.X, ALU.add)
+            nc.vector.tensor_reduce(least[:, v], auc_t[:].rearrange("p (v d) -> p v d", d=D), AX.X, ALU.min)
+
+        ln_conc = keep.tile([P, S // D], F32, name="ln_conc")
+        result = keep.tile([P, S // D], F32, name="result")
+        nc.scalar.activation(ln_conc[:], conc[:], ACT.Ln, scale=0.7, bias=0.05)
+        nc.vector.scalar_tensor_tensor(result[:], least[:], 0.5, ln_conc[:], ALU.mult, ALU.add)
+        nc.sync.dma_start(out, result[:])

@@ -24,9 +24,9 @@ PACK = 4
 TILES = S // P
 CHUNK = 256
 CHUNKS = S // CHUNK
-HALF = 512
 LN_FLOOR = 2.0 ** -62
-RECIP_V = 32
+RECIP_V = 28
+GROUPS = [[0,1,2,3],[4,5],[6,7]]
 
 
 def tile_picked_ypkpd_logc_p_kernel(tc, x_words, x_scales, w1, w2, ago, amt, offs, out):
@@ -42,98 +42,137 @@ def tile_picked_ypkpd_logc_p_kernel(tc, x_words, x_scales, w1, w2, ago, amt, off
         ago_col = keep.tile([P, TILES], F32, name="ago_col")
         amt_col = keep.tile([P, TILES], F32, name="amt_col")
 
-        nc.vector.memset(scale_table[:].bitcast(I32), 0)
+        nc.gpsimd.memset(scale_table[:, : T // 2].bitcast(I32), 0)
+        nc.vector.memset(scale_table[:, T // 2 :].bitcast(I32), 0)
+        nc.sync.dma_start(offsets[:], offs)
+        nc.sync.dma_start(w_raw[0][:], w1.rearrange("(p j) n -> p j n", j=PACK))
         for q in range(4):
             nc.sync.dma_start(scale_table[32 * q : 32 * q + 4, :].bitcast(I32), x_scales[0, 4 * q : 4 * q + 4, :].bitcast(I32))
-        nc.sync.dma_start(offsets[:], offs)
-        for h, w in enumerate((w1, w2)):
-            nc.sync.dma_start(w_raw[h][:], w.rearrange("(p j) n -> p j n", j=PACK))
         nc.sync.dma_start(word_table[:].bitcast(I32), x_words[0].rearrange("p c r -> p (c r)").bitcast(I32))
+        nc.sync.dma_start(w_raw[1][:], w2.rearrange("(p j) n -> p j n", j=PACK))
         with nc.allow_non_contiguous_dma(reason="one value a partition and tile"):
             nc.sync.dma_start(ago_col[:], ago[0].rearrange("(t p) -> p t", p=P))
             nc.sync.dma_start(amt_col[:], amt[0].rearrange("(t p) -> p t", p=P))
 
         warm_in = keep.tile([P, 1], F32, name="warm_in")
         warm_out = keep.tile([P, 1], F32, name="warm_out")
-        nc.gpsimd.memset(warm_in[:], 0.0)
+        nc.vector.memset(warm_in[:], 0.0)
         nc.scalar.activation(warm_out[:], warm_in[:], ACT.Sigmoid)
 
         ident = keep.tile([P, P], F32, name="ident")
         make_identity(nc, ident[:])
 
-        w_bf = keep.tile([P, 2, N, PACK], BF16, name="w_bf", align_bytes=64)
-        for h in range(2):
-            nc.scalar.activation(w_bf[:, h, :, :], w_raw[h][:].rearrange("p j n -> p n j"), ACT.Copy)
-        w_codes = keep.tile([P, 2 * N], U32, name="w_codes", align_bytes=64)
-        w_scales = keep.tile([P, 2 * N], U8, name="w_scales", align_bytes=64)
-
         x_scale = keep.tile([P, S], U8, name="x_scale", align_bytes=64)
         nc.vector.tensor_copy(x_scale[:], scale_table[:].indirect(offsets[:]))
-        nc.vector.quantize_mx(out=w_codes[:].bitcast(FP8X4), scales=w_scales[:], in_=w_bf[:].rearrange("p h n j -> p (h n j)"))
+
+        def quantise(h, tag):
+            w_bf = keep.tile([P, N, PACK], BF16, name="w_bf%d" % h, tag=tag, align_bytes=64)
+            nc.scalar.activation(w_bf[:], w_raw[h][:].rearrange("p j n -> p n j"), ACT.Copy)
+            codes = keep.tile([P, N], U32, name="w_codes%d" % h, align_bytes=64)
+            scales = keep.tile([P, N], U8, name="w_scales%d" % h, align_bytes=64)
+            nc.vector.quantize_mx(out=codes[:].bitcast(FP8X4), scales=scales[:], in_=w_bf[:].rearrange("p n j -> p (n j)"))
+            return codes, scales
+
+        u = keep.tile([P, 2, TILES, N], F32, name="u")
+        x_code = {}
+        y = {}
+
+        def gather(c):
+            x_code[c] = keep.tile([P, CHUNK], U32, name="x_code%d" % c, tag="x_code%d" % c, align_bytes=64)
+            nc.vector.tensor_copy(x_code[c][:], word_table[:].indirect(offsets[:, c * CHUNK // 16 : (c + 1) * CHUNK // 16]))
+
+        def product(h, c, w_q):
+            bank = psum.tile([P, 2, N], F32, name="y%d%d" % (h, c), tag="bank%d" % (h * CHUNKS + c))
+            y[h, c] = bank
+            for i in range(2):
+                nc.tensor.matmul_mx(
+                    out=bank[:, i, :],
+                    lhsT=x_code[c][:, i * P : (i + 1) * P].bitcast(FP8X4),
+                    lhsT_scale=x_scale[:, c * CHUNK + i * P : c * CHUNK + (i + 1) * P],
+                    rhs=w_q[0][:].bitcast(FP8X4),
+                    rhs_scale=w_q[1][:],
+                    start=True,
+                    stop=True,
+                )
+            nc.scalar.activation(u[:, h, 2 * c : 2 * c + 2, :], bank[:], ACT.Sigmoid, scale=-1.0)
+
+        w1_q = quantise(0, "w_bf0")
+        gather(0)
+        gather(1)
+        w2_q = quantise(1, "x_code2")
+        product(0, 0, w1_q)
+        product(0, 1, w1_q)
+        product(1, 0, w2_q)
+        product(1, 1, w2_q)
+        for c in range(2, CHUNKS):
+            gather(c)
+            product(0, c, w1_q)
+            product(1, c, w2_q)
 
         neg_ago = keep.tile([P, TILES], F32, name="neg_ago")
         neg_ago4 = keep.tile([P, TILES], F32, name="neg_ago4")
         nc.gpsimd.tensor_scalar(neg_ago[:], ago_col[:], -1.0, 0.0, ALU.mult, ALU.add)
         nc.gpsimd.tensor_scalar(neg_ago4[:], ago_col[:], -0.4, 0.0, ALU.mult, ALU.add)
 
-        u = keep.tile([P, 2, TILES, N], F32, name="u")
-        y = []
-        for c in range(CHUNKS):
-            x_code = keep.tile([P, CHUNK], U32, name="x_code%d" % c, align_bytes=64)
-            nc.vector.tensor_copy(x_code[:], word_table[:].indirect(offsets[:, c * CHUNK // 16 : (c + 1) * CHUNK // 16]))
-            bank = psum.tile([P, 2, 2, N], F32, name="y%d" % c)
-            y.append(bank)
-            for i in range(2):
-                nc.tensor.matmul_mx(
-                    out=bank[:, i, :, :].rearrange("p h n -> p (h n)"),
-                    lhsT=x_code[:, i * P : (i + 1) * P].bitcast(FP8X4),
-                    lhsT_scale=x_scale[:, c * CHUNK + i * P : c * CHUNK + (i + 1) * P],
-                    rhs=w_codes[:].bitcast(FP8X4),
-                    rhs_scale=w_scales[:],
-                    start=True,
-                    stop=True,
-                )
-            nc.scalar.activation(u[:, :, 2 * c : 2 * c + 2, :].rearrange("p h i n -> p i h n"), bank[:], ACT.Sigmoid, scale=-1.0)
-
-        for h in range(2):
-            nc.scalar.activation(u[:, h, :, :], u[:, h, :, :], ACT.Ln, bias=LN_FLOOR)
+        floor = keep.tile([P, 2], F32, name="floor")
+        nc.vector.tensor_scalar(floor[:], u[:, :, TILES - 1, N - 1], 0.0, LN_FLOOR, ALU.mult, ALU.add)
         for h in range(2):
             for c in range(CHUNKS):
                 piece = u[:, h, 2 * c : 2 * c + 2, :]
-                nc.vector.scalar_tensor_tensor(piece, piece, -1.0, y[c][:, :, h, :], ALU.mult, ALU.max)
+                nc.scalar.activation(piece, piece, ACT.Ln, bias=floor[:, 0:1])
+                nc.vector.scalar_tensor_tensor(piece, piece, -1.0, y[h, c][:], ALU.mult, ALU.max)
+                if (h, c) == (1, 0):
+                    fast_v = keep.tile([P, TILES, RECIP_V], F32, name="fast_v")
+                    nc.vector.tensor_scalar(fast_v[:], u[:, 0, :, :RECIP_V], 0.4, None, ALU.add)
 
         inv = keep.tile([P, TILES, N], F32, name="inv")
-        fast_v = keep.tile([P, TILES, RECIP_V], F32, name="fast_v")
         ln_fast = keep.tile([P, TILES, N - RECIP_V], F32, name="ln_fast")
         nc.scalar.activation(ln_fast[:], u[:, 0, :, RECIP_V:], ACT.Ln, bias=0.4)
-        nc.vector.tensor_scalar(fast_v[:], u[:, 0, :, :RECIP_V], 0.4, None, ALU.add)
         nc.vector.reciprocal(inv[:, :, :RECIP_V], fast_v[:])
 
         scaled = keep.tile([P, TILES, 2, N], F32, name="scaled")
         neg_auc = keep.tile([P, TILES, N], F32, name="neg_auc")
         conc = keep.tile([P, S // D], F32, name="conc")
         least = keep.tile([P, S // D], F32, name="least")
-        per_half = TILES // 2
-        for half in range(2):
-            dose_t = psum.tile([P, HALF], F32, name="dose_t%d" % half)
-            auc_t = psum.tile([P, HALF], F32, name="auc_t%d" % half)
-            for i in range(per_half):
-                t = half * per_half + i
-                col = slice(t, t + 1)
-                nc.scalar.activation(u[:, 0, t, :], u[:, 0, t, :], ACT.Exp, scale=neg_ago[:, col], bias=neg_ago4[:, col])
-                nc.scalar.activation(u[:, 1, t, :], u[:, 1, t, :], ACT.Exp, scale=neg_ago4[:, col], bias=math.log(0.3 / 0.7))
-                if i == 0:
-                    tiles = slice(half * per_half, (half + 1) * per_half)
-                    nc.scalar.activation(inv[:, tiles, RECIP_V:], ln_fast[:, tiles, :], ACT.Exp, scale=-1.0)
-                nc.vector.tensor_scalar(scaled[:, t, :, :], u[:, :, t, :], amt_col[:, col], None, ALU.mult)
-                nc.vector.scalar_tensor_tensor(neg_auc[:, t, :], scaled[:, t, 0, :], amt_col[:, col], inv[:, t, :], ALU.subtract, ALU.mult)
-                cols = slice(i * P, (i + 1) * P)
-                for h in range(2):
-                    nc.tensor.matmul(dose_t[:, cols], scaled[:, t, h, :], ident[:], start=(h == 0), stop=(h == 1), is_transpose=True)
-                nc.tensor.transpose(auc_t[:, cols], neg_auc[:, t, :], ident[:])
-            v = slice(half * P, (half + 1) * P)
-            nc.vector.tensor_reduce(conc[:, v], dose_t[:].rearrange("p (v d) -> p v d", d=D), AX.X, ALU.add)
-            nc.vector.tensor_reduce(least[:, v], auc_t[:].rearrange("p (v d) -> p v d", d=D), AX.X, ALU.min)
+        group_of = {t: g for g, tiles in enumerate(GROUPS) for t in tiles}
+        dose_t = [psum.tile([P, len(tiles) * P], F32, name="dose_t%d" % g, tag="bank%d" % (2 * g)) for g, tiles in enumerate(GROUPS)]
+        auc_t = [psum.tile([P, len(tiles) * P], F32, name="auc_t%d" % g, tag="bank%d" % (2 * g + 1)) for g, tiles in enumerate(GROUPS)]
+
+        def decay(t):
+            col = slice(t, t + 1)
+            g = group_of[t]
+            cols = slice((t - GROUPS[g][0]) * P, (t - GROUPS[g][0] + 1) * P)
+            nc.scalar.activation(u[:, 0, t, :], u[:, 0, t, :], ACT.Exp, scale=neg_ago[:, col], bias=neg_ago4[:, col])
+            nc.scalar.activation(u[:, 1, t, :], u[:, 1, t, :], ACT.Exp, scale=neg_ago4[:, col], bias=math.log(0.3 / 0.7))
+            if t % (TILES // 2) == 0:
+                tiles = slice(t, t + TILES // 2)
+                nc.scalar.activation(inv[:, tiles, RECIP_V:], ln_fast[:, tiles, :], ACT.Exp, scale=-1.0)
+            nc.vector.tensor_scalar(scaled[:, t, :, :], u[:, :, t, :], amt_col[:, col], None, ALU.mult)
+            for h in range(2):
+                nc.tensor.matmul(dose_t[g][:, cols], scaled[:, t, h, :], ident[:], start=(h == 0), stop=(h == 1), is_transpose=True)
+
+        def exposure(t):
+            g = group_of[t]
+            cols = slice((t - GROUPS[g][0]) * P, (t - GROUPS[g][0] + 1) * P)
+            nc.vector.scalar_tensor_tensor(neg_auc[:, t, :], scaled[:, t, 0, :], amt_col[:, t : t + 1], inv[:, t, :], ALU.subtract, ALU.mult)
+            nc.tensor.transpose(auc_t[g][:, cols], neg_auc[:, t, :], ident[:])
+
+        def patients(g):
+            return slice(GROUPS[g][0] * P // D, (GROUPS[g][-1] + 1) * P // D)
+
+        def fold(g):
+            nc.vector.tensor_reduce(conc[:, patients(g)], dose_t[g][:].rearrange("p (v d) -> p v d", d=D), AX.X, ALU.add)
+            nc.vector.tensor_reduce(least[:, patients(g)], auc_t[g][:].rearrange("p (v d) -> p v d", d=D), AX.X, ALU.min)
+
+        for t in range(TILES + 1):
+            if t < TILES:
+                decay(t)
+            if t > 0:
+                exposure(t - 1)
+            if t == GROUPS[1][0] + 1:
+                fold(0)
+        for g in range(1, len(GROUPS)):
+            fold(g)
 
         ln_conc = keep.tile([P, S // D], F32, name="ln_conc")
         result = keep.tile([P, S // D], F32, name="result")

@@ -25,7 +25,8 @@ TILES = S // P
 CHUNK = 256
 CHUNKS = S // CHUNK
 LN_FLOOR = 2.0 ** -62
-RECIP_V = 28
+RECIP_V = 416
+INV_AFTER = {1: (RECIP_V, 768), 3: (768, S)}
 GROUPS = [[0,1,2,3],[4,5],[6,7]]
 
 
@@ -39,8 +40,7 @@ def tile_picked_ypkpd_logc_p_kernel(tc, x_words, x_scales, w1, w2, ago, amt, off
         scale_table = keep.tile([P, T], U8, name="scale_table", align_bytes=64)
         word_table = keep.tile([P, T], U32, name="word_table", align_bytes=64)
         w_raw = [keep.tile([P, PACK, N], F32, name="w_raw%d" % h) for h in range(2)]
-        ago_col = keep.tile([P, TILES], F32, name="ago_col")
-        amt_col = keep.tile([P, TILES], F32, name="amt_col")
+        dose_rows = keep.tile([P, P], F32, name="dose_rows")
 
         nc.gpsimd.memset(scale_table[:, : T // 2].bitcast(I32), 0)
         nc.vector.memset(scale_table[:, T // 2 :].bitcast(I32), 0)
@@ -48,11 +48,11 @@ def tile_picked_ypkpd_logc_p_kernel(tc, x_words, x_scales, w1, w2, ago, amt, off
         nc.sync.dma_start(w_raw[0][:], w1.rearrange("(p j) n -> p j n", j=PACK))
         for q in range(4):
             nc.sync.dma_start(scale_table[32 * q : 32 * q + 4, :].bitcast(I32), x_scales[0, 4 * q : 4 * q + 4, :].bitcast(I32))
-        nc.sync.dma_start(word_table[:].bitcast(I32), x_words[0].rearrange("p c r -> p (c r)").bitcast(I32))
         nc.sync.dma_start(w_raw[1][:], w2.rearrange("(p j) n -> p j n", j=PACK))
-        with nc.allow_non_contiguous_dma(reason="one value a partition and tile"):
-            nc.sync.dma_start(ago_col[:], ago[0].rearrange("(t p) -> p t", p=P))
-            nc.sync.dma_start(amt_col[:], amt[0].rearrange("(t p) -> p t", p=P))
+        nc.sync.dma_start(word_table[:].bitcast(I32), x_words[0].rearrange("p c r -> p (c r)").bitcast(I32))
+        nc.gpsimd.memset(dose_rows[:], 0.0)
+        nc.sync.dma_start(dose_rows[:TILES, :], ago[0].rearrange("(t p) -> t p", p=P))
+        nc.sync.dma_start(dose_rows[TILES : 2 * TILES, :], amt[0].rearrange("(t p) -> t p", p=P))
 
         warm_in = keep.tile([P, 1], F32, name="warm_in")
         warm_out = keep.tile([P, 1], F32, name="warm_out")
@@ -65,13 +65,16 @@ def tile_picked_ypkpd_logc_p_kernel(tc, x_words, x_scales, w1, w2, ago, amt, off
         x_scale = keep.tile([P, S], U8, name="x_scale", align_bytes=64)
         nc.vector.tensor_copy(x_scale[:], scale_table[:].indirect(offsets[:]))
 
-        def quantise(h, tag):
-            w_bf = keep.tile([P, N, PACK], BF16, name="w_bf%d" % h, tag=tag, align_bytes=64)
-            nc.scalar.activation(w_bf[:], w_raw[h][:].rearrange("p j n -> p n j"), ACT.Copy)
-            codes = keep.tile([P, N], U32, name="w_codes%d" % h, align_bytes=64)
-            scales = keep.tile([P, N], U8, name="w_scales%d" % h, align_bytes=64)
-            nc.vector.quantize_mx(out=codes[:].bitcast(FP8X4), scales=scales[:], in_=w_bf[:].rearrange("p n j -> p (n j)"))
-            return codes, scales
+        w_bf = keep.tile([P, 2, N, PACK], BF16, name="w_bf", align_bytes=64)
+        for h in range(2):
+            nc.scalar.activation(w_bf[:, h, :, :], w_raw[h][:].rearrange("p j n -> p n j"), ACT.Copy)
+        w_codes = keep.tile([P, 2, N], U32, name="w_codes", align_bytes=64)
+        w_scales = keep.tile([P, 2, N], U8, name="w_scales", align_bytes=64)
+        nc.vector.quantize_mx(
+            out=w_codes[:].rearrange("p h n -> p (h n)").bitcast(FP8X4),
+            scales=w_scales[:].rearrange("p h n -> p (h n)"),
+            in_=w_bf[:].rearrange("p h n j -> p (h n j)"),
+        )
 
         u = keep.tile([P, 2, TILES, N], F32, name="u")
         x_code = {}
@@ -81,7 +84,7 @@ def tile_picked_ypkpd_logc_p_kernel(tc, x_words, x_scales, w1, w2, ago, amt, off
             x_code[c] = keep.tile([P, CHUNK], U32, name="x_code%d" % c, tag="x_code%d" % c, align_bytes=64)
             nc.vector.tensor_copy(x_code[c][:], word_table[:].indirect(offsets[:, c * CHUNK // 16 : (c + 1) * CHUNK // 16]))
 
-        def product(h, c, w_q):
+        def product(h, c):
             bank = psum.tile([P, 2, N], F32, name="y%d%d" % (h, c), tag="bank%d" % (h * CHUNKS + c))
             y[h, c] = bank
             for i in range(2):
@@ -89,46 +92,61 @@ def tile_picked_ypkpd_logc_p_kernel(tc, x_words, x_scales, w1, w2, ago, amt, off
                     out=bank[:, i, :],
                     lhsT=x_code[c][:, i * P : (i + 1) * P].bitcast(FP8X4),
                     lhsT_scale=x_scale[:, c * CHUNK + i * P : c * CHUNK + (i + 1) * P],
-                    rhs=w_q[0][:].bitcast(FP8X4),
-                    rhs_scale=w_q[1][:],
+                    rhs=w_codes[:, h, :].bitcast(FP8X4),
+                    rhs_scale=w_scales[:, h, :],
                     start=True,
                     stop=True,
                 )
             nc.scalar.activation(u[:, h, 2 * c : 2 * c + 2, :], bank[:], ACT.Sigmoid, scale=-1.0)
 
-        w1_q = quantise(0, "w_bf0")
-        gather(0)
-        gather(1)
-        w2_q = quantise(1, "x_code2")
-        product(0, 0, w1_q)
-        product(0, 1, w1_q)
-        product(1, 0, w2_q)
-        product(1, 1, w2_q)
-        for c in range(2, CHUNKS):
+        for c in range(CHUNKS):
             gather(c)
-            product(0, c, w1_q)
-            product(1, c, w2_q)
-
-        neg_ago = keep.tile([P, TILES], F32, name="neg_ago")
-        neg_ago4 = keep.tile([P, TILES], F32, name="neg_ago4")
-        nc.gpsimd.tensor_scalar(neg_ago[:], ago_col[:], -1.0, 0.0, ALU.mult, ALU.add)
-        nc.gpsimd.tensor_scalar(neg_ago4[:], ago_col[:], -0.4, 0.0, ALU.mult, ALU.add)
+            product(0, c)
+            product(1, c)
 
         floor = keep.tile([P, 2], F32, name="floor")
         nc.vector.tensor_scalar(floor[:], u[:, :, TILES - 1, N - 1], 0.0, LN_FLOOR, ALU.mult, ALU.add)
-        for h in range(2):
-            for c in range(CHUNKS):
-                piece = u[:, h, 2 * c : 2 * c + 2, :]
-                nc.scalar.activation(piece, piece, ACT.Ln, bias=floor[:, 0:1])
-                nc.vector.scalar_tensor_tensor(piece, piece, -1.0, y[h, c][:], ALU.mult, ALU.max)
-                if (h, c) == (1, 0):
-                    fast_v = keep.tile([P, TILES, RECIP_V], F32, name="fast_v")
-                    nc.vector.tensor_scalar(fast_v[:], u[:, 0, :, :RECIP_V], 0.4, None, ALU.add)
+        def softplus(h, c):
+            piece = u[:, h, 2 * c : 2 * c + 2, :]
+            nc.scalar.activation(piece, piece, ACT.Ln, bias=floor[:, 0:1])
+            nc.vector.scalar_tensor_tensor(piece, piece, -1.0, y[h, c][:], ALU.mult, ALU.max)
 
-        inv = keep.tile([P, TILES, N], F32, name="inv")
-        ln_fast = keep.tile([P, TILES, N - RECIP_V], F32, name="ln_fast")
-        nc.scalar.activation(ln_fast[:], u[:, 0, :, RECIP_V:], ACT.Ln, bias=0.4)
-        nc.vector.reciprocal(inv[:, :, :RECIP_V], fast_v[:])
+        for c in range(CHUNKS):
+            softplus(0, c)
+
+        dose_cols_t = psum.tile([P, P], F32, name="dose_cols_t", tag="bank0")
+        nc.tensor.transpose(dose_cols_t[:], dose_rows[:], ident[:])
+        dose_cols = keep.tile([P, 2, TILES], F32, name="dose_cols")
+        neg_ago = keep.tile([P, TILES], F32, name="neg_ago")
+        neg_ago4 = keep.tile([P, TILES], F32, name="neg_ago4")
+        amt_col = dose_cols[:, 1, :]
+
+        half, quarter = RECIP_V // 2, RECIP_V // 4
+        soft_fast = u[:, 0, :, :].rearrange("p t n -> p (t n)")
+        inv = keep.tile([P, S], F32, name="inv")
+        fast = keep.tile([P, RECIP_V], F32, name="fast")
+        pair = keep.tile([P, half], F32, name="pair")
+        quad = keep.tile([P, quarter], F32, name="quad")
+        inv_quad = keep.tile([P, quarter], F32, name="inv_quad")
+        inv_pair = keep.tile([P, half], F32, name="inv_pair")
+        nc.vector.tensor_scalar(fast[:], soft_fast[:, :RECIP_V], 0.4, None, ALU.add)
+        nc.vector.tensor_copy(dose_cols[:].rearrange("p a t -> p (a t)"), dose_cols_t[:, : 2 * TILES])
+        nc.gpsimd.tensor_scalar(neg_ago[:], dose_cols[:, 0, :], -1.0, 0.0, ALU.mult, ALU.add)
+        nc.gpsimd.tensor_scalar(neg_ago4[:], dose_cols[:, 0, :], -0.4, 0.0, ALU.mult, ALU.add)
+        nc.vector.tensor_tensor(pair[:], fast[:, :half], fast[:, half:], ALU.mult)
+        softplus(1, 0)
+        nc.vector.tensor_tensor(quad[:], pair[:, :quarter], pair[:, quarter:], ALU.mult)
+        softplus(1, 1)
+        nc.vector.reciprocal(inv_quad[:], quad[:])
+        softplus(1, 2)
+        nc.vector.tensor_tensor(inv_pair[:, :quarter], inv_quad[:], pair[:, quarter:], ALU.mult)
+        nc.vector.tensor_tensor(inv_pair[:, quarter:], inv_quad[:], pair[:, :quarter], ALU.mult)
+        softplus(1, 3)
+        nc.vector.tensor_tensor(inv[:, :half], inv_pair[:], fast[:, half:], ALU.mult)
+        nc.vector.tensor_tensor(inv[:, half:RECIP_V], inv_pair[:], fast[:, :half], ALU.mult)
+
+        ln_fast = keep.tile([P, S - RECIP_V], F32, name="ln_fast")
+        nc.scalar.activation(ln_fast[:], soft_fast[:, RECIP_V:], ACT.Ln, bias=0.4)
 
         scaled = keep.tile([P, TILES, 2, N], F32, name="scaled")
         neg_auc = keep.tile([P, TILES, N], F32, name="neg_auc")
@@ -144,9 +162,9 @@ def tile_picked_ypkpd_logc_p_kernel(tc, x_words, x_scales, w1, w2, ago, amt, off
             cols = slice((t - GROUPS[g][0]) * P, (t - GROUPS[g][0] + 1) * P)
             nc.scalar.activation(u[:, 0, t, :], u[:, 0, t, :], ACT.Exp, scale=neg_ago[:, col], bias=neg_ago4[:, col])
             nc.scalar.activation(u[:, 1, t, :], u[:, 1, t, :], ACT.Exp, scale=neg_ago4[:, col], bias=math.log(0.3 / 0.7))
-            if t % (TILES // 2) == 0:
-                tiles = slice(t, t + TILES // 2)
-                nc.scalar.activation(inv[:, tiles, RECIP_V:], ln_fast[:, tiles, :], ACT.Exp, scale=-1.0)
+            if t in INV_AFTER:
+                lo, hi = INV_AFTER[t]
+                nc.scalar.activation(inv[:, lo:hi], ln_fast[:, lo - RECIP_V : hi - RECIP_V], ACT.Exp, scale=-1.0)
             nc.vector.tensor_scalar(scaled[:, t, :, :], u[:, :, t, :], amt_col[:, col], None, ALU.mult)
             for h in range(2):
                 nc.tensor.matmul(dose_t[g][:, cols], scaled[:, t, h, :], ident[:], start=(h == 0), stop=(h == 1), is_transpose=True)
@@ -154,7 +172,7 @@ def tile_picked_ypkpd_logc_p_kernel(tc, x_words, x_scales, w1, w2, ago, amt, off
         def exposure(t):
             g = group_of[t]
             cols = slice((t - GROUPS[g][0]) * P, (t - GROUPS[g][0] + 1) * P)
-            nc.vector.scalar_tensor_tensor(neg_auc[:, t, :], scaled[:, t, 0, :], amt_col[:, t : t + 1], inv[:, t, :], ALU.subtract, ALU.mult)
+            nc.vector.scalar_tensor_tensor(neg_auc[:, t, :], scaled[:, t, 0, :], amt_col[:, t : t + 1], inv[:, t * N : (t + 1) * N], ALU.subtract, ALU.mult)
             nc.tensor.transpose(auc_t[g][:, cols], neg_auc[:, t, :], ident[:])
 
         def patients(g):
@@ -176,6 +194,7 @@ def tile_picked_ypkpd_logc_p_kernel(tc, x_words, x_scales, w1, w2, ago, amt, off
 
         ln_conc = keep.tile([P, S // D], F32, name="ln_conc")
         result = keep.tile([P, S // D], F32, name="result")
-        nc.scalar.activation(ln_conc[:], conc[:], ACT.Ln, scale=0.7, bias=0.05)
-        nc.vector.scalar_tensor_tensor(result[:], least[:], 0.5, ln_conc[:], ALU.mult, ALU.add)
-        nc.sync.dma_start(out, result[:])
+        for v in (slice(0, P), slice(P, 2 * P)):
+            nc.scalar.activation(ln_conc[:, v], conc[:, v], ACT.Ln, scale=0.7, bias=0.05)
+            nc.vector.scalar_tensor_tensor(result[:, v], least[:, v], 0.5, ln_conc[:, v], ALU.mult, ALU.add)
+            nc.sync.dma_start(out[:, v], result[:, v])

import math
from contextlib import ExitStack

import concourse.mybir as mybir
from concourse.masks import make_identity

K, T, S, D, N = 512, 2048, 1024, 4, 128
FLOPS = 2 * 2 * K * N * S
BYTES = K * T + K // 32 * T + 2 * K * N * 4 + 2 * S * 4 + 128 * S // 16 * 2 + N * S // D * 4

F32 = mybir.dt.float32
BF16 = mybir.dt.bfloat16
I32 = mybir.dt.int32
U32 = mybir.dt.uint32
U16 = mybir.dt.uint16
U8 = mybir.dt.uint8
FP8X4 = mybir.dt.float8_e4m3fn_x4
ACT = mybir.ActivationFunctionType
ALU = mybir.AluOpType
AX = mybir.AxisListType

P = 128
PACK = 4
TILES = S // P
CHUNK = 256
CHUNKS = S // CHUNK
LN_FLOOR = 2.0 ** -62
RECIP_V = 416
INV_AFTER = {1: (RECIP_V, 768), 3: (768, S)}
GROUPS = [[0,1,2,3],[4,5],[6,7]]


def tile_picked_ypkpd_logc_p_kernel(tc, x_words, x_scales, w1, w2, ago, amt, offs, out):
    nc = tc.nc
    with ExitStack() as ctx:
        keep = ctx.enter_context(tc.tile_pool(name="keep", bufs=1))
        psum = ctx.enter_context(tc.psum_pool(name="psum", bufs=1))

        offsets = keep.tile([P, S // 16], U16, name="offsets")
        scale_table = keep.tile([P, T], U8, name="scale_table", align_bytes=64)
        word_table = keep.tile([P, T], U32, name="word_table", align_bytes=64)
        w_raw = [keep.tile([P, PACK, N], F32, name="w_raw%d" % h) for h in range(2)]
        dose_rows = keep.tile([P, P], F32, name="dose_rows")

        nc.gpsimd.memset(scale_table[:, : T // 2].bitcast(I32), 0)
        nc.vector.memset(scale_table[:, T // 2 :].bitcast(I32), 0)
        nc.sync.dma_start(offsets[:], offs)
        nc.sync.dma_start(w_raw[0][:], w1.rearrange("(p j) n -> p j n", j=PACK))
        for q in range(4):
            nc.sync.dma_start(scale_table[32 * q : 32 * q + 4, :].bitcast(I32), x_scales[0, 4 * q : 4 * q + 4, :].bitcast(I32))
        nc.sync.dma_start(w_raw[1][:], w2.rearrange("(p j) n -> p j n", j=PACK))
        nc.sync.dma_start(word_table[:].bitcast(I32), x_words[0].rearrange("p c r -> p (c r)").bitcast(I32))
        nc.gpsimd.memset(dose_rows[:], 0.0)
        nc.sync.dma_start(dose_rows[:TILES, :], ago[0].rearrange("(t p) -> t p", p=P))
        nc.sync.dma_start(dose_rows[TILES : 2 * TILES, :], amt[0].rearrange("(t p) -> t p", p=P))

        warm_in = keep.tile([P, 1], F32, name="warm_in")
        warm_out = keep.tile([P, 1], F32, name="warm_out")
        nc.vector.memset(warm_in[:], 0.0)
        nc.scalar.activation(warm_out[:], warm_in[:], ACT.Sigmoid)

        ident = keep.tile([P, P], F32, name="ident")
        make_identity(nc, ident[:])

        x_scale = keep.tile([P, S], U8, name="x_scale", align_bytes=64)
        nc.vector.tensor_copy(x_scale[:], scale_table[:].indirect(offsets[:]))

        w_bf = keep.tile([P, 2, N, PACK], BF16, name="w_bf", align_bytes=64)
        for h in range(2):
            nc.scalar.activation(w_bf[:, h, :, :], w_raw[h][:].rearrange("p j n -> p n j"), ACT.Copy)
        w_codes = keep.tile([P, 2, N], U32, name="w_codes", align_bytes=64)
        w_scales = keep.tile([P, 2, N], U8, name="w_scales", align_bytes=64)
        nc.vector.quantize_mx(
            out=w_codes[:].rearrange("p h n -> p (h n)").bitcast(FP8X4),
            scales=w_scales[:].rearrange("p h n -> p (h n)"),
            in_=w_bf[:].rearrange("p h n j -> p (h n j)"),
        )

        u = keep.tile([P, 2, TILES, N], F32, name="u")
        x_code = {}
        y = {}

        def gather(c):
            x_code[c] = keep.tile([P, CHUNK], U32, name="x_code%d" % c, tag="x_code%d" % c, align_bytes=64)
            nc.vector.tensor_copy(x_code[c][:], word_table[:].indirect(offsets[:, c * CHUNK // 16 : (c + 1) * CHUNK // 16]))

        def product(h, c):
            bank = psum.tile([P, 2, N], F32, name="y%d%d" % (h, c), tag="bank%d" % (h * CHUNKS + c))
            y[h, c] = bank
            for i in range(2):
                nc.tensor.matmul_mx(
                    out=bank[:, i, :],
                    lhsT=x_code[c][:, i * P : (i + 1) * P].bitcast(FP8X4),
                    lhsT_scale=x_scale[:, c * CHUNK + i * P : c * CHUNK + (i + 1) * P],
                    rhs=w_codes[:, h, :].bitcast(FP8X4),
                    rhs_scale=w_scales[:, h, :],
                    start=True,
                    stop=True,
                )
            nc.scalar.activation(u[:, h, 2 * c : 2 * c + 2, :], bank[:], ACT.Sigmoid, scale=-1.0)

        for c in range(CHUNKS):
            gather(c)
            product(0, c)
            product(1, c)

        floor = keep.tile([P, 2], F32, name="floor")
        nc.vector.tensor_scalar(floor[:], u[:, :, TILES - 1, N - 1], 0.0, LN_FLOOR, ALU.mult, ALU.add)
        def softplus(h, c):
            piece = u[:, h, 2 * c : 2 * c + 2, :]
            nc.scalar.activation(piece, piece, ACT.Ln, bias=floor[:, 0:1])
            nc.vector.scalar_tensor_tensor(piece, piece, -1.0, y[h, c][:], ALU.mult, ALU.max)

        for c in range(CHUNKS):
            softplus(0, c)

        dose_cols_t = psum.tile([P, P], F32, name="dose_cols_t", tag="bank0")
        nc.tensor.transpose(dose_cols_t[:], dose_rows[:], ident[:])
        dose_cols = keep.tile([P, 2, TILES], F32, name="dose_cols")
        neg_ago = keep.tile([P, TILES], F32, name="neg_ago")
        neg_ago4 = keep.tile([P, TILES], F32, name="neg_ago4")
        amt_col = dose_cols[:, 1, :]

        half, quarter = RECIP_V // 2, RECIP_V // 4
        soft_fast = u[:, 0, :, :].rearrange("p t n -> p (t n)")
        inv = keep.tile([P, S], F32, name="inv")
        fast = keep.tile([P, RECIP_V], F32, name="fast")
        pair = keep.tile([P, half], F32, name="pair")
        quad = keep.tile([P, quarter], F32, name="quad")
        inv_quad = keep.tile([P, quarter], F32, name="inv_quad")
        inv_pair = keep.tile([P, half], F32, name="inv_pair")
        nc.vector.tensor_scalar(fast[:], soft_fast[:, :RECIP_V], 0.4, None, ALU.add)
        nc.vector.tensor_copy(dose_cols[:].rearrange("p a t -> p (a t)"), dose_cols_t[:, : 2 * TILES])
        nc.gpsimd.tensor_scalar(neg_ago[:], dose_cols[:, 0, :], -1.0, 0.0, ALU.mult, ALU.add)
        nc.gpsimd.tensor_scalar(neg_ago4[:], dose_cols[:, 0, :], -0.4, 0.0, ALU.mult, ALU.add)
        nc.vector.tensor_tensor(pair[:], fast[:, :half], fast[:, half:], ALU.mult)
        softplus(1, 0)
        nc.vector.tensor_tensor(quad[:], pair[:, :quarter], pair[:, quarter:], ALU.mult)
        softplus(1, 1)
        nc.vector.reciprocal(inv_quad[:], quad[:])
        softplus(1, 2)
        nc.vector.tensor_tensor(inv_pair[:, :quarter], inv_quad[:], pair[:, quarter:], ALU.mult)
        nc.vector.tensor_tensor(inv_pair[:, quarter:], inv_quad[:], pair[:, :quarter], ALU.mult)
        softplus(1, 3)
        nc.vector.tensor_tensor(inv[:, :half], inv_pair[:], fast[:, half:], ALU.mult)
        nc.vector.tensor_tensor(inv[:, half:RECIP_V], inv_pair[:], fast[:, :half], ALU.mult)

        ln_fast = keep.tile([P, S - RECIP_V], F32, name="ln_fast")
        nc.scalar.activation(ln_fast[:], soft_fast[:, RECIP_V:], ACT.Ln, bias=0.4)

        scaled = keep.tile([P, TILES, 2, N], F32, name="scaled")
        neg_auc = keep.tile([P, TILES, N], F32, name="neg_auc")
        conc = keep.tile([P, S // D], F32, name="conc")
        least = keep.tile([P, S // D], F32, name="least")
        group_of = {t: g for g, tiles in enumerate(GROUPS) for t in tiles}
        dose_t = [psum.tile([P, len(tiles) * P], F32, name="dose_t%d" % g, tag="bank%d" % (2 * g)) for g, tiles in enumerate(GROUPS)]
        auc_t = [psum.tile([P, len(tiles) * P], F32, name="auc_t%d" % g, tag="bank%d" % (2 * g + 1)) for g, tiles in enumerate(GROUPS)]

        def decay(t):
            col = slice(t, t + 1)
            g = group_of[t]
            cols = slice((t - GROUPS[g][0]) * P, (t - GROUPS[g][0] + 1) * P)
            nc.scalar.activation(u[:, 0, t, :], u[:, 0, t, :], ACT.Exp, scale=neg_ago[:, col], bias=neg_ago4[:, col])
            nc.scalar.activation(u[:, 1, t, :], u[:, 1, t, :], ACT.Exp, scale=neg_ago4[:, col], bias=math.log(0.3 / 0.7))
            if t in INV_AFTER:
                lo, hi = INV_AFTER[t]
                nc.scalar.activation(inv[:, lo:hi], ln_fast[:, lo - RECIP_V : hi - RECIP_V], ACT.Exp, scale=-1.0)
            nc.vector.tensor_scalar(scaled[:, t, :, :], u[:, :, t, :], amt_col[:, col], None, ALU.mult)
            for h in range(2):
                nc.tensor.matmul(dose_t[g][:, cols], scaled[:, t, h, :], ident[:], start=(h == 0), stop=(h == 1), is_transpose=True)

        def exposure(t):
            g = group_of[t]
            cols = slice((t - GROUPS[g][0]) * P, (t - GROUPS[g][0] + 1) * P)
            nc.vector.scalar_tensor_tensor(neg_auc[:, t, :], scaled[:, t, 0, :], amt_col[:, t : t + 1], inv[:, t * N : (t + 1) * N], ALU.subtract, ALU.mult)
            nc.tensor.transpose(auc_t[g][:, cols], neg_auc[:, t, :], ident[:])

        def patients(g):
            return slice(GROUPS[g][0] * P // D, (GROUPS[g][-1] + 1) * P // D)

        def fold(g):
            nc.vector.tensor_reduce(conc[:, patients(g)], dose_t[g][:].rearrange("p (v d) -> p v d", d=D), AX.X, ALU.add)
            nc.vector.tensor_reduce(least[:, patients(g)], auc_t[g][:].rearrange("p (v d) -> p v d", d=D), AX.X, ALU.min)

        for t in range(TILES + 1):
            if t < TILES:
                decay(t)
            if t > 0:
                exposure(t - 1)
            if t == GROUPS[1][0] + 1:
                fold(0)
        for g in range(1, len(GROUPS)):
            fold(g)

        ln_conc = keep.tile([P, S // D], F32, name="ln_conc")
        result = keep.tile([P, S // D], F32, name="result")
        for v in (slice(0, P), slice(P, 2 * P)):
            nc.scalar.activation(ln_conc[:, v], conc[:, v], ACT.Ln, scale=0.7, bias=0.05)
            nc.vector.scalar_tensor_tensor(result[:, v], least[:, v], 0.5, ln_conc[:, v], ALU.mult, ALU.add)
            nc.sync.dma_start(out[:, v], result[:, v])
